import numpy as np
import ml_dtypes


def mxq(x, axis, fmt="e4m3"):
    dtype, down = {"e4m3": (ml_dtypes.float8_e4m3fn, 7), "e5m2": (ml_dtypes.float8_e5m2, 14)}[fmt]
    v = np.moveaxis(np.asarray(x, np.float32).astype(ml_dtypes.bfloat16).astype(np.float64), axis, -1)
    blocks = v.reshape(v.shape[:-1] + (-1, 32))
    amax = np.abs(blocks).max(-1, keepdims=True)
    byte = np.maximum(np.where(amax > 0, np.frexp(amax)[1] - 1 + 127, 0) - down, 1)
    scale = np.exp2(byte - 127.0)
    codes = (blocks / scale).astype(np.float32).astype(dtype).astype(np.float64)
    return np.moveaxis((codes * scale).reshape(v.shape), -1, axis)


WIDE = False


def mx_kscale(k):
    if not WIDE:
        return np.ones(k)
    levels = np.array([24, -24, 12, -12, 0])
    if k % 512:
        return np.exp2(np.random.permutation(np.resize(levels, k // 32))).repeat(32)
    a = np.empty((k // 512, 16))
    for p in range(k // 512):
        a[p, :8] = np.random.permutation(np.resize(levels, 8))
        for g in range(8):
            far = levels[np.abs(levels - a[p, g]) >= 10]
            a[p, g + 8] = far[np.random.randint(len(far))]
    return np.exp2(a.ravel()).repeat(32)


def f64(x):
    return np.asarray(x).astype(np.float64)


def striped8(idx):
    return np.concatenate([v.reshape(-1, 16).T for v in idx]).astype(np.uint16)


def unstriped8(offs):
    return np.stack([offs[16 * g:16 * g + 16].T.reshape(-1) for g in range(8)]).astype(np.int64)


E2M1 = np.array([0.0, 0.5, 1.0, 1.5, 2.0, 3.0, 4.0, 6.0, -0.0, -0.5, -1.0, -1.5, -2.0, -3.0, -4.0, -6.0])


def pack_weight(w, fmt):
    k, n = w.shape
    w = f64(np.asarray(w, np.float32).astype(ml_dtypes.bfloat16)).reshape(k // 32, 32, n)
    amax = np.abs(w).max(1)
    if fmt == "e4m3":
        byte = np.frexp(amax)[1] - 1 + 127 - 7
    else:
        mant, ex = np.frexp(amax / 6.0)
        byte = np.where(mant > 0.5, ex, ex - 1) + 127
    byte = np.clip(np.where(amax > 0, byte, 1), 1, 254)
    scaled = (w * np.exp2(127.0 - byte)[:, None, :]).reshape(k, n).astype(np.float32)
    by_word = np.ascontiguousarray(scaled.reshape(k // 512, 128, 4, n).transpose(0, 1, 3, 2))
    if fmt == "e4m3":
        words = by_word.astype(ml_dtypes.float8_e4m3fn).view(np.uint8)
    else:
        c = by_word.astype(ml_dtypes.float4_e2m1fn).view(np.uint8) & 0xF
        words = (c[..., 0::2] | (c[..., 1::2] << 4)).reshape(k // 512, 128, 2 * n)
    return np.ascontiguousarray(words), np.ascontiguousarray(byte.astype(np.uint8).reshape(k // 512, 16, n))


def unpack_weight(words, scales, fmt):
    g, _, n = scales.shape
    words = np.ascontiguousarray(words).reshape(g, 128, n, -1)
    if fmt == "e4m3":
        vals = words.view(ml_dtypes.float8_e4m3fn).astype(np.float64)
    else:
        nib = np.empty((g, 128, n, 4), np.uint8)
        nib[..., 0::2] = words & 0xF
        nib[..., 1::2] = words >> 4
        vals = E2M1[nib]
    vals = vals * np.repeat(np.exp2(scales.astype(np.float64) - 127.0), 8, axis=1)[..., None]
    return vals.transpose(0, 1, 3, 2).reshape(g * 512, n)


K, L, N, T, J = 1024, 512, 512, 2048, 1024


def setup_inputs():
    n = np.random.standard_normal
    s = mx_kscale(K)[:, None]
    s2 = mx_kscale(L)[:, None]
    p_wx = pack_weight(n((L, N)) / np.sqrt(L) / s2, "e2m1")
    return {
        "xT": (n((K, T)) * s).astype(np.float32),
        "wgt": np.repeat(np.random.uniform(0.5, 2.0, (8, J)), 16, axis=0).astype(np.float32),
        "wt": (n((K, N)) / np.sqrt(K) / s).astype(np.float32),
        "c": (n((L, J)) * s2).astype(np.float32),
        "wx_words": p_wx[0],
        "wx_scales": p_wx[1],
        "wgo": np.repeat(np.random.uniform(0.5, 2.0, (8, J)), 16, axis=0).astype(np.float32),
        "offs": striped8(np.stack([np.random.permutation(T)[:J] for _ in range(8)])),
        "offs2": striped8(np.stack([np.random.permutation(T)[:J] for _ in range(8)])),
    }


def reference(xT, wgt, wt, c, wx_words, wx_scales, wgo, offs, offs2):
    idx = unstriped8(offs)
    idx2 = unstriped8(offs2)
    rows = np.arange(K)
    xg = f64(wgt)[rows // 4 % 128] * f64(xT)[rows[:, None], idx[rows % 512 // 64]]
    xT_ = mxq(xg, 0, "e4m3")
    wt_ = mxq(f64(wt), 0, "e4m3")
    c_q_ = mxq(f64(c), 0, "e4m3")
    c_r_ = mxq(f64(c) - c_q_, 0, "e4m3")
    wx_ = unpack_weight(wx_words, wx_scales, "e2m1")
    y = wt_.T @ xT_ + wx_.T @ c_q_ + wx_.T @ c_r_
    out = np.zeros((N, T))
    rows = np.arange(N)
    out[rows[:, None], idx2[rows % 128 // 16]] = f64(wgo)[rows % 128] * (y)
    return out

@@ -1,0 +1,204 @@
+from contextlib import ExitStack
+
+import concourse.mybir as mybir
+from concourse.masks import make_identity
+
+K, L, N, T, J = 1024, 512, 512, 2048, 1024
+FLOPS = 2 * (K + 2 * L) * N * J
+
+F32 = mybir.dt.float32
+BF16 = mybir.dt.bfloat16
+I32 = mybir.dt.int32
+U32 = mybir.dt.uint32
+U16 = mybir.dt.uint16
+U8 = mybir.dt.uint8
+FP8X4 = mybir.dt.float8_e4m3fn_x4
+FP4X4 = mybir.dt.float4_e2m1fn_x4
+MULT = mybir.AluOpType.mult
+SUBTRACT = mybir.AluOpType.subtract
+
+P = 128
+PACK = 4
+K_PASS = P * PACK
+PASSES = K // K_PASS
+HALF = 512
+HALVES = J // HALF
+LIST_COLS = HALF // 16
+BLOCKS = N // P
+CHUNK = 128
+
+
+def tile_list_scat_kernel(
+    tc, xT, wgt, wt, c, wx_words, wx_scales, wgo, offs, offs2, out
+):
+    nc = tc.nc
+    with ExitStack() as ctx:
+        keep = ctx.enter_context(tc.tile_pool(name="keep", bufs=1))
+        work = ctx.enter_context(tc.tile_pool(name="work", bufs=1))
+        psum = ctx.enter_context(tc.psum_pool(name="psum", bufs=4))
+
+        def walk_rows(ap):
+            return ap.rearrange("p t (c i) -> p c t i", i=PACK)
+
+        def walk_words(ap):
+            return ap.rearrange("p (c i) t -> p c t i", i=PACK)
+
+        def operand(name, width):
+            codes = keep.tile([P, width], U32, name=name + "_codes", align_bytes=64)
+            scales = keep.tile([P, width], U8, name=name + "_scales", align_bytes=64)
+            return codes, scales
+
+        def staged(name):
+            return work.tile([P, HALF, PACK], BF16, name=name, tag="staged", bufs=6, align_bytes=64)
+
+        def quantize(dst, src):
+            nc.vector.quantize_mx(
+                out=dst[0][:].bitcast(FP8X4), scales=dst[1][:], in_=src[:].rearrange("p w t -> p (w t)")
+            )
+
+        def half_cols(h):
+            return slice(h * HALF, (h + 1) * HALF)
+
+        def list_cols(h):
+            return slice(h * LIST_COLS, (h + 1) * LIST_COLS)
+
+        pages = [keep.tile([P, T], F32, name="page%d" % b) for b in range(BLOCKS)]
+        for b in range(BLOCKS):
+            nc.vector.memset(pages[b][:], 0.0)
+
+        shifted = keep.tile([P, 2 * PACK - 1, P], BF16, name="shifted")
+        nc.gpsimd.memset(shifted[:], 0.0)
+        make_identity(nc, shifted[:, PACK - 1, :], nomemset=True)
+        wx_plane = keep.tile([P, N], U8, name="wx_plane", align_bytes=64)
+        nc.gpsimd.memset(wx_plane[:].bitcast(I32), 0)
+        eye_staged = staged("eye_staged")
+        for i in range(PACK):
+            first = PACK - 1 - i
+            nc.scalar.copy(
+                out=eye_staged[:, i * P : (i + 1) * P, :],
+                in_=shifted[:, first : first + PACK, :].rearrange("p t m -> p m t"),
+            )
+        eye = operand("eye", K_PASS)
+        quantize(eye, eye_staged)
+
+        gather_list = keep.tile([P, J // 16], U16, name="gather_list")
+        scatter_list = keep.tile([P, J // 16], U16, name="scatter_list")
+        wgt_sb = [keep.tile([P, HALF], F32, name="wgt%d" % h) for h in range(HALVES)]
+        wgo_sb = [keep.tile([P, HALF], F32, name="wgo%d" % h) for h in range(HALVES)]
+        wx_sb = keep.tile([P, 2 * N], U8, name="wx_sb", align_bytes=64)
+        x_rows = xT.rearrange("(a p i) t -> a i p t", p=P, i=PACK)
+        wt_rows = wt.rearrange("(a p i) n -> a p i n", p=P, i=PACK)
+        c_rows = c.rearrange("(p i) j -> p i j", i=PACK)
+
+        picked = {}
+        xg, wq, cq, cr, acc = {}, {}, {}, {}, {}
+
+        def load_plane(q):
+            plane = work.tile([P, T], F32, name="plane%d" % q, tag="plane", bufs=6)
+            nc.sync.dma_start(out=plane[:], in_=x_rows[q // PACK, q % PACK])
+            return plane
+
+        def gather(q, h, plane):
+            a, i = divmod(q, PACK)
+            if i == 0:
+                picked[a, h] = keep.tile([P, PACK, HALF], F32, name="picked%d_%d" % (a, h))
+            nc.vector.tensor_tensor(
+                picked[a, h][:, i, :], plane[:].indirect(gather_list[:, list_cols(h)]), wgt_sb[h][:], MULT
+            )
+
+        def quantize_rows(name, rows):
+            st = staged(name + "_staged")
+            nc.scalar.copy(out=walk_words(st[:]), in_=walk_rows(rows[:]))
+            dst = operand(name, HALF)
+            quantize(dst, st)
+            return dst
+
+        def weights(a):
+            raw = keep.tile([P, PACK, N], F32, name="wt_raw%d" % a)
+            nc.sync.dma_start(out=raw[:], in_=wt_rows[a])
+            wq[a] = quantize_rows("wq%d" % a, raw)
+
+        def tiers(h):
+            raw = keep.tile([P, PACK, HALF], F32, name="c_raw%d" % h)
+            nc.sync.dma_start(out=raw[:], in_=c_rows[:, :, half_cols(h)])
+            cq[h] = quantize_rows("cq%d" % h, raw)
+            st = staged("cr_staged%d" % h)
+            for u in range(HALF // CHUNK):
+                cols = slice(u * CHUNK, (u + 1) * CHUNK)
+                back = psum.tile([P, PACK, CHUNK], F32, name="back%d_%d" % (h, u), tag="back")
+                for i in range(PACK):
+                    rows = slice(i * P, (i + 1) * P)
+                    nc.tensor.matmul_mx(
+                        out=back[:, i, :],
+                        lhsT=eye[0][:, rows].bitcast(FP8X4),
+                        lhsT_scale=eye[1][:, rows],
+                        rhs=cq[h][0][:, cols].bitcast(FP8X4),
+                        rhs_scale=cq[h][1][:, cols],
+                        start=True,
+                        stop=True,
+                    )
+                nc.vector.tensor_tensor(
+                    walk_words(st[:, cols, :]), walk_rows(raw[:, :, cols]), walk_rows(back[:]), SUBTRACT
+                )
+            cr[h] = operand("cr%d" % h, HALF)
+            quantize(cr[h], st)
+
+        def product(b, h):
+            cols = slice(b * P, (b + 1) * P)
+            bank = psum.tile([P, HALF], F32, name="acc%d_%d" % (b, h), tag="acc")
+            wx_block = (wx_sb[:, 2 * b * P : 2 * (b + 1) * P].bitcast(FP4X4), wx_plane[:, cols])
+            terms = [(wx_block, cq[h]), (wx_block, cr[h])]
+            for a in range(PASSES):
+                terms.append(((wq[a][0][:, cols].bitcast(FP8X4), wq[a][1][:, cols]), xg[a, h]))
+            for s, (left, right) in enumerate(terms):
+                nc.tensor.matmul_mx(
+                    out=bank[:],
+                    lhsT=left[0],
+                    lhsT_scale=left[1],
+                    rhs=right[0][:].bitcast(FP8X4),
+                    rhs_scale=right[1][:],
+                    start=(s == 0),
+                    stop=(s == len(terms) - 1),
+                )
+            y = work.tile([P, HALF], F32, name="y%d_%d" % (b, h), tag="y", bufs=4)
+            nc.scalar.copy(out=y[:], in_=bank[:])
+            nc.vector.tensor_tensor(pages[b][:].indirect(scatter_list[:, list_cols(h)]), y[:], wgo_sb[h][:], MULT)
+
+        def plane_step(q):
+            plane = load_plane(q)
+            if q == 0:
+                nc.sync.dma_start(out=wgt_sb[1][:], in_=wgt[:, half_cols(1)])
+            for h in range(HALVES):
+                gather(q, h, plane)
+                if q % PACK == PACK - 1:
+                    a = q // PACK
+                    xg[a, h] = quantize_rows("xg%d_%d" % (a, h), picked[a, h])
+
+        nc.sync.dma_start(gather_list[:], offs)
+        nc.sync.dma_start(out=wgt_sb[0][:], in_=wgt[:, half_cols(0)])
+        plane_step(0)
+        tiers(0)
+        plane_step(1)
+        plane_step(2)
+        nc.sync.dma_start(scatter_list[:], offs2)
+        nc.sync.dma_start(out=wx_sb[:].bitcast(I32), in_=wx_words[0].bitcast(I32))
+        for quad in range(4):
+            nc.sync.dma_start(
+                out=wx_plane[32 * quad : 32 * quad + 4, :].bitcast(I32),
+                in_=wx_scales[0, 4 * quad : 4 * quad + 4, :].bitcast(I32),
+            )
+        plane_step(3)
+        weights(0)
+        plane_step(4)
+        plane_step(5)
+        weights(1)
+        plane_step(6)
+        plane_step(7)
+        nc.sync.dma_start(out=wgo_sb[0][:], in_=wgo[:, half_cols(0)])
+        for b in range(BLOCKS):
+            product(b, 0)
+        tiers(1)
+        nc.sync.dma_start(out=wgo_sb[1][:], in_=wgo[:, half_cols(1)])
+        for b in range(BLOCKS):
+            product(b, 1)
+            nc.sync.dma_start(out=out[b * P : (b + 1) * P, :], in_=pages[b][:])

@@ -48,8 +48,8 @@ def tile_list_scat_kernel(
             scales = keep.tile([P, width], U8, name=name + "_scales", align_bytes=64)
             return codes, scales
 
-        def staged(name):
-            return work.tile([P, HALF, PACK], BF16, name=name, tag="staged", bufs=6, align_bytes=64)
+        def staged(name, slot):
+            return keep.tile([P, HALF, PACK], BF16, name=name, tag="staged_" + slot, align_bytes=64)
 
         def quantize(dst, src):
             nc.vector.quantize_mx(
@@ -71,7 +71,7 @@ def tile_list_scat_kernel(
         make_identity(nc, shifted[:, PACK - 1, :], nomemset=True)
         wx_plane = keep.tile([P, N], U8, name="wx_plane", align_bytes=64)
         nc.gpsimd.memset(wx_plane[:].bitcast(I32), 0)
-        eye_staged = staged("eye_staged")
+        eye_staged = staged("eye_staged", "xg0_0")
         for i in range(PACK):
             first = PACK - 1 - i
             nc.scalar.copy(
@@ -83,7 +83,7 @@ def tile_list_scat_kernel(
 
         gather_list = keep.tile([P, J // 16], U16, name="gather_list")
         scatter_list = keep.tile([P, J // 16], U16, name="scatter_list")
-        wgt_sb = [keep.tile([P, HALF], F32, name="wgt%d" % h) for h in range(HALVES)]
+        wgt_sb = [keep.tile([P, HALF], F32, name="wgt0", tag="late"), keep.tile([P, HALF], F32, name="wgt1")]
         wgo_sb = [keep.tile([P, HALF], F32, name="wgo%d" % h) for h in range(HALVES)]
         wx_sb = keep.tile([P, 2 * N], U8, name="wx_sb", align_bytes=64)
         x_rows = xT.rearrange("(a p i) t -> a i p t", p=P, i=PACK)
@@ -91,7 +91,7 @@ def tile_list_scat_kernel(
         c_rows = c.rearrange("(p i) j -> p i j", i=PACK)
 
         picked = {}
-        xg, wq, cq, cr, acc = {}, {}, {}, {}, {}
+        xg, wq, cq, cr, c_raw, planes = {}, {}, {}, {}, {}, {}
 
         def load_plane(q):
             plane = work.tile([P, T], F32, name="plane%d" % q, tag="plane", bufs=6)
@@ -101,13 +101,14 @@ def tile_list_scat_kernel(
         def gather(q, h, plane):
             a, i = divmod(q, PACK)
             if i == 0:
-                picked[a, h] = keep.tile([P, PACK, HALF], F32, name="picked%d_%d" % (a, h))
+                tag = "late" if (a, h) == (1, 1) else "picked%d_%d" % (a, h)
+                picked[a, h] = keep.tile([P, PACK, HALF], F32, name="picked%d_%d" % (a, h), tag=tag)
             nc.vector.tensor_tensor(
                 picked[a, h][:, i, :], plane[:].indirect(gather_list[:, list_cols(h)]), wgt_sb[h][:], MULT
             )
 
-        def quantize_rows(name, rows):
-            st = staged(name + "_staged")
+        def quantize_rows(name, rows, slot):
+            st = staged(name + "_staged", slot)
             nc.scalar.copy(out=walk_words(st[:]), in_=walk_rows(rows[:]))
             dst = operand(name, HALF)
             quantize(dst, st)
@@ -116,13 +117,17 @@ def tile_list_scat_kernel(
         def weights(a):
             raw = keep.tile([P, PACK, N], F32, name="wt_raw%d" % a)
             nc.sync.dma_start(out=raw[:], in_=wt_rows[a])
-            wq[a] = quantize_rows("wq%d" % a, raw)
+            wq[a] = quantize_rows("wq%d" % a, raw, "wq%d" % a)
 
-        def tiers(h):
+        def first_tier(h):
             raw = keep.tile([P, PACK, HALF], F32, name="c_raw%d" % h)
             nc.sync.dma_start(out=raw[:], in_=c_rows[:, :, half_cols(h)])
-            cq[h] = quantize_rows("cq%d" % h, raw)
-            st = staged("cr_staged%d" % h)
+            cq[h] = quantize_rows("cq%d" % h, raw, "cq")
+            c_raw[h] = raw
+
+        def second_tier(h, slot):
+            raw = c_raw[h]
+            st = staged("cr_staged%d" % h, slot)
             for u in range(HALF // CHUNK):
                 cols = slice(u * CHUNK, (u + 1) * CHUNK)
                 back = psum.tile([P, PACK, CHUNK], F32, name="back%d_%d" % (h, u), tag="back")
@@ -160,26 +165,32 @@ def tile_list_scat_kernel(
                     start=(s == 0),
                     stop=(s == len(terms) - 1),
                 )
-            y = work.tile([P, HALF], F32, name="y%d_%d" % (b, h), tag="y", bufs=4)
+            y = work.tile([P, HALF], F32, name="y%d_%d" % (b, h), tag="y", bufs=8)
             nc.scalar.copy(out=y[:], in_=bank[:])
             nc.vector.tensor_tensor(pages[b][:].indirect(scatter_list[:, list_cols(h)]), y[:], wgo_sb[h][:], MULT)
 
-        def plane_step(q):
-            plane = load_plane(q)
-            if q == 0:
-                nc.sync.dma_start(out=wgt_sb[1][:], in_=wgt[:, half_cols(1)])
-            for h in range(HALVES):
-                gather(q, h, plane)
-                if q % PACK == PACK - 1:
-                    a = q // PACK
-                    xg[a, h] = quantize_rows("xg%d_%d" % (a, h), picked[a, h])
+        def quantize_picked(a, h):
+            xg[a, h] = quantize_rows("xg%d_%d" % (a, h), picked[a, h], "xg%d_%d" % (a, h))
 
         nc.sync.dma_start(gather_list[:], offs)
         nc.sync.dma_start(out=wgt_sb[0][:], in_=wgt[:, half_cols(0)])
-        plane_step(0)
-        tiers(0)
-        plane_step(1)
-        plane_step(2)
+        for q in range(3):
+            planes[q] = load_plane(q)
+            if q == 0:
+                nc.sync.dma_start(out=wgt_sb[1][:], in_=wgt[:, half_cols(1)])
+            for h in range(HALVES):
+                gather(q, h, planes[q])
+        first_tier(0)
+        planes[3] = load_plane(3)
+        for h in range(HALVES):
+            gather(3, h, planes[3])
+        planes[4] = load_plane(4)
+        gather(4, 0, planes[4])
+        second_tier(0, "cr0")
+        for h in range(HALVES):
+            quantize_picked(0, h)
+        planes[5] = load_plane(5)
+        gather(5, 0, planes[5])
         nc.sync.dma_start(scatter_list[:], offs2)
         nc.sync.dma_start(out=wx_sb[:].bitcast(I32), in_=wx_words[0].bitcast(I32))
         for quad in range(4):
@@ -187,18 +198,21 @@ def tile_list_scat_kernel(
                 out=wx_plane[32 * quad : 32 * quad + 4, :].bitcast(I32),
                 in_=wx_scales[0, 4 * quad : 4 * quad + 4, :].bitcast(I32),
             )
-        plane_step(3)
         weights(0)
-        plane_step(4)
-        plane_step(5)
+        first_tier(1)
+        for q in range(6, 8):
+            planes[q] = load_plane(q)
+            gather(q, 0, planes[q])
+        quantize_picked(1, 0)
         weights(1)
-        plane_step(6)
-        plane_step(7)
-        nc.sync.dma_start(out=wgo_sb[0][:], in_=wgo[:, half_cols(0)])
-        for b in range(BLOCKS):
-            product(b, 0)
-        tiers(1)
-        nc.sync.dma_start(out=wgo_sb[1][:], in_=wgo[:, half_cols(1)])
-        for b in range(BLOCKS):
-            product(b, 1)
-            nc.sync.dma_start(out=out[b * P : (b + 1) * P, :], in_=pages[b][:])
+        for q in range(4, 8):
+            gather(q, 1, planes[q])
+        second_tier(1, "wq1")
+        quantize_picked(1, 1)
+        for h in range(HALVES):
+            nc.sync.dma_start(out=wgo_sb[h][:], in_=wgo[:, half_cols(h)])
+        for h in range(HALVES):
+            for b in range(BLOCKS):
+                product(b, h)
+                if h == HALVES - 1:
+                    nc.sync.dma_start(out=out[b * P : (b + 1) * P, :], in_=pages[b][:])

@@ -23,9 +23,17 @@ K_PASS = P * PACK
 PASSES = K // K_PASS
 HALF = 512
 HALVES = J // HALF
-LIST_COLS = HALF // 16
+QUARTER = HALF // 2
+CHUNK = HALF // PACK
+CHUNKS = HALF // CHUNK
 BLOCKS = N // P
-CHUNK = 128
+GROUP = 16
+QUADRANT = 32
+SCALE_ROWS = 4
+
+
+def span(index, width):
+    return slice(index * width, (index + 1) * width)
 
 
 def tile_list_scat_kernel(
@@ -34,185 +42,200 @@ def tile_list_scat_kernel(
     nc = tc.nc
     with ExitStack() as ctx:
         keep = ctx.enter_context(tc.tile_pool(name="keep", bufs=1))
-        work = ctx.enter_context(tc.tile_pool(name="work", bufs=1))
-        psum = ctx.enter_context(tc.psum_pool(name="psum", bufs=4))
+        psum = ctx.enter_context(tc.psum_pool(name="psum", bufs=1))
 
-        def walk_rows(ap):
-            return ap.rearrange("p t (c i) -> p c t i", i=PACK)
+        def sbuf(name, shape, dtype, after=None):
+            return keep.tile([P] + shape, dtype, name=name, tag=after or name, align_bytes=64)
 
-        def walk_words(ap):
-            return ap.rearrange("p (c i) t -> p c t i", i=PACK)
+        def operand(name, width, after=None):
+            return sbuf(name + "_codes", [width], U32, after), sbuf(name + "_scales", [width], U8)
 
-        def operand(name, width):
-            codes = keep.tile([P, width], U32, name=name + "_codes", align_bytes=64)
-            scales = keep.tile([P, width], U8, name=name + "_scales", align_bytes=64)
-            return codes, scales
+        def staging(name, width, after=None):
+            return sbuf(name + "_staging", [width, PACK], BF16, after)[:]
 
-        def staged(name, slot):
-            return keep.tile([P, HALF, PACK], BF16, name=name, tag="staged_" + slot, align_bytes=64)
+        def as_staging(row):
+            return row.bitcast(BF16).rearrange("p (w t) -> p w t", t=PACK)
 
-        def quantize(dst, src):
+        def walk_rows(rows):
+            return rows.rearrange("p t (c i) -> p c t i", i=PACK)
+
+        def walk_staging(staged):
+            return staged.rearrange("p (c i) t -> p c t i", i=PACK)
+
+        def weave(staged, rows):
+            nc.scalar.copy(out=walk_staging(staged), in_=walk_rows(rows))
+
+        def quantize(dst, cols, staged):
             nc.vector.quantize_mx(
-                out=dst[0][:].bitcast(FP8X4), scales=dst[1][:], in_=src[:].rearrange("p w t -> p (w t)")
+                out=dst[0][:, cols].bitcast(FP8X4), scales=dst[1][:, cols], in_=staged.rearrange("p w t -> p (w t)")
             )
 
-        def half_cols(h):
-            return slice(h * HALF, (h + 1) * HALF)
+        def list_cols(cols):
+            return slice(cols.start // GROUP, cols.stop // GROUP)
 
-        def list_cols(h):
-            return slice(h * LIST_COLS, (h + 1) * LIST_COLS)
+        gather_list = sbuf("gather_list", [J // GROUP], U16)
+        scatter_list = sbuf("scatter_list", [J // GROUP], U16)
+        wgt_sb = sbuf("wgt_sb", [J], F32)
+        wgo_sb = sbuf("wgo_sb", [J], F32)
+        wx_codes = sbuf("wx_codes", [2 * N], U8)
+        wx_plane = sbuf("wx_plane", [N], U8)
+        picked = [sbuf("picked%d" % a, [PACK, J], F32) for a in range(PASSES)]
+        x_planes = xT.rearrange("(a p t) w -> a t p w", p=P, t=PACK)
+        wt_rows = wt.rearrange("(a p t) n -> a p t n", p=P, t=PACK)
+        c_rows = c.rearrange("(p t) j -> p t j", t=PACK)
 
-        pages = [keep.tile([P, T], F32, name="page%d" % b) for b in range(BLOCKS)]
-        for b in range(BLOCKS):
-            nc.vector.memset(pages[b][:], 0.0)
-
-        shifted = keep.tile([P, 2 * PACK - 1, P], BF16, name="shifted")
-        nc.gpsimd.memset(shifted[:], 0.0)
-        make_identity(nc, shifted[:, PACK - 1, :], nomemset=True)
-        wx_plane = keep.tile([P, N], U8, name="wx_plane", align_bytes=64)
-        nc.gpsimd.memset(wx_plane[:].bitcast(I32), 0)
-        eye_staged = staged("eye_staged", "xg0_0")
-        for i in range(PACK):
-            first = PACK - 1 - i
-            nc.scalar.copy(
-                out=eye_staged[:, i * P : (i + 1) * P, :],
-                in_=shifted[:, first : first + PACK, :].rearrange("p t m -> p m t"),
-            )
+        diagonals = sbuf("diagonals", [2 * PACK - 1, P], BF16)
+        nc.vector.memset(diagonals[:], 0.0)
+        make_identity(nc, diagonals[:, PACK - 1, :], nomemset=True)
         eye = operand("eye", K_PASS)
-        quantize(eye, eye_staged)
+        eye_staging = staging("eye", K_PASS)
+        for t in range(PACK):
+            first = PACK - 1 - t
+            nc.scalar.copy(
+                out=eye_staging[:, span(t, P), :],
+                in_=diagonals[:, first : first + PACK, :].rearrange("p t m -> p m t"),
+            )
+        quantize(eye, span(0, K_PASS), eye_staging)
 
-        gather_list = keep.tile([P, J // 16], U16, name="gather_list")
-        scatter_list = keep.tile([P, J // 16], U16, name="scatter_list")
-        wgt_sb = [keep.tile([P, HALF], F32, name="wgt0", tag="late"), keep.tile([P, HALF], F32, name="wgt1")]
-        wgo_sb = [keep.tile([P, HALF], F32, name="wgo%d" % h) for h in range(HALVES)]
-        wx_sb = keep.tile([P, 2 * N], U8, name="wx_sb", align_bytes=64)
-        x_rows = xT.rearrange("(a p i) t -> a i p t", p=P, i=PACK)
-        wt_rows = wt.rearrange("(a p i) n -> a p i n", p=P, i=PACK)
-        c_rows = c.rearrange("(p i) j -> p i j", i=PACK)
-
-        picked = {}
-        xg, wq, cq, cr, c_raw, planes = {}, {}, {}, {}, {}, {}
+        nc.gpsimd.memset(wx_plane[:].bitcast(I32), 0)
+        pages = [sbuf("page%d" % b, [T], F32) for b in range(BLOCKS)]
+        for page in pages:
+            nc.vector.memset(page[:], 0.0)
 
         def load_plane(q):
-            plane = work.tile([P, T], F32, name="plane%d" % q, tag="plane", bufs=6)
-            nc.sync.dma_start(out=plane[:], in_=x_rows[q // PACK, q % PACK])
+            plane = sbuf("plane%d" % q, [T], F32)
+            nc.sync.dma_start(out=plane[:], in_=x_planes[q // PACK, q % PACK])
             return plane
 
-        def gather(q, h, plane):
-            a, i = divmod(q, PACK)
-            if i == 0:
-                tag = "late" if (a, h) == (1, 1) else "picked%d_%d" % (a, h)
-                picked[a, h] = keep.tile([P, PACK, HALF], F32, name="picked%d_%d" % (a, h), tag=tag)
+        def gather(q, plane, cols):
             nc.vector.tensor_tensor(
-                picked[a, h][:, i, :], plane[:].indirect(gather_list[:, list_cols(h)]), wgt_sb[h][:], MULT
+                picked[q // PACK][:, q % PACK, cols],
+                plane[:].indirect(gather_list[:, list_cols(cols)]),
+                wgt_sb[:, cols],
+                MULT,
             )
 
-        def quantize_rows(name, rows, slot):
-            st = staged(name + "_staged", slot)
-            nc.scalar.copy(out=walk_words(st[:]), in_=walk_rows(rows[:]))
-            dst = operand(name, HALF)
-            quantize(dst, st)
-            return dst
+        def load_rows(name, rows):
+            tile = sbuf(name, [PACK, HALF], F32)
+            nc.sync.dma_start(out=tile[:], in_=rows)
+            return tile
 
-        def weights(a):
-            raw = keep.tile([P, PACK, N], F32, name="wt_raw%d" % a)
-            nc.sync.dma_start(out=raw[:], in_=wt_rows[a])
-            wq[a] = quantize_rows("wq%d" % a, raw, "wq%d" % a)
+        def load_wx_scales(quadrants):
+            for quadrant in quadrants:
+                start = QUADRANT * quadrant
+                nc.sync.dma_start(
+                    out=wx_plane[start : start + SCALE_ROWS, :].bitcast(I32),
+                    in_=wx_scales[0, span(quadrant, SCALE_ROWS), :].bitcast(I32),
+                )
 
-        def first_tier(h):
-            raw = keep.tile([P, PACK, HALF], F32, name="c_raw%d" % h)
-            nc.sync.dma_start(out=raw[:], in_=c_rows[:, :, half_cols(h)])
-            cq[h] = quantize_rows("cq%d" % h, raw, "cq")
-            c_raw[h] = raw
-
-        def second_tier(h, slot):
-            raw = c_raw[h]
-            st = staged("cr_staged%d" % h, slot)
-            for u in range(HALF // CHUNK):
-                cols = slice(u * CHUNK, (u + 1) * CHUNK)
-                back = psum.tile([P, PACK, CHUNK], F32, name="back%d_%d" % (h, u), tag="back")
-                for i in range(PACK):
-                    rows = slice(i * P, (i + 1) * P)
+        def remainder(h, c_half, staged):
+            for u in range(CHUNKS):
+                cols = span(h * CHUNKS + u, CHUNK)
+                back = psum.tile([P, PACK, CHUNK], F32, name="back%d_%d" % (h, u), tag="back%d" % u)
+                for t in range(PACK):
                     nc.tensor.matmul_mx(
-                        out=back[:, i, :],
-                        lhsT=eye[0][:, rows].bitcast(FP8X4),
-                        lhsT_scale=eye[1][:, rows],
-                        rhs=cq[h][0][:, cols].bitcast(FP8X4),
-                        rhs_scale=cq[h][1][:, cols],
+                        out=back[:, t, :],
+                        lhsT=eye[0][:, span(t, P)].bitcast(FP8X4),
+                        lhsT_scale=eye[1][:, span(t, P)],
+                        rhs=cq[0][:, cols].bitcast(FP8X4),
+                        rhs_scale=cq[1][:, cols],
                         start=True,
                         stop=True,
                     )
                 nc.vector.tensor_tensor(
-                    walk_words(st[:, cols, :]), walk_rows(raw[:, :, cols]), walk_rows(back[:]), SUBTRACT
+                    walk_staging(staged[:, span(u, CHUNK), :]),
+                    walk_rows(c_half[:, :, span(u, CHUNK)]),
+                    walk_rows(back[:]),
+                    SUBTRACT,
                 )
-            cr[h] = operand("cr%d" % h, HALF)
-            quantize(cr[h], st)
 
         def product(b, h):
-            cols = slice(b * P, (b + 1) * P)
-            bank = psum.tile([P, HALF], F32, name="acc%d_%d" % (b, h), tag="acc")
-            wx_block = (wx_sb[:, 2 * b * P : 2 * (b + 1) * P].bitcast(FP4X4), wx_plane[:, cols])
-            terms = [(wx_block, cq[h]), (wx_block, cr[h])]
+            rows, cols = span(b, P), span(h, HALF)
+            wx_block = (wx_codes[:, span(b, 2 * P)].bitcast(FP4X4), wx_plane[:, rows])
+            terms = [(wx_block, cq), (wx_block, cr)]
             for a in range(PASSES):
-                terms.append(((wq[a][0][:, cols].bitcast(FP8X4), wq[a][1][:, cols]), xg[a, h]))
+                terms.append(((wq[a][0][:, rows].bitcast(FP8X4), wq[a][1][:, rows]), xg[a]))
+            acc = psum.tile([P, HALF], F32, name="acc%d_%d" % (b, h), tag="acc%d" % b)
             for s, (left, right) in enumerate(terms):
                 nc.tensor.matmul_mx(
-                    out=bank[:],
+                    out=acc[:],
                     lhsT=left[0],
                     lhsT_scale=left[1],
-                    rhs=right[0][:].bitcast(FP8X4),
-                    rhs_scale=right[1][:],
+                    rhs=right[0][:, cols].bitcast(FP8X4),
+                    rhs_scale=right[1][:, cols],
                     start=(s == 0),
                     stop=(s == len(terms) - 1),
                 )
-            y = work.tile([P, HALF], F32, name="y%d_%d" % (b, h), tag="y", bufs=8)
-            nc.scalar.copy(out=y[:], in_=bank[:])
-            nc.vector.tensor_tensor(pages[b][:].indirect(scatter_list[:, list_cols(h)]), y[:], wgo_sb[h][:], MULT)
+            y = sbuf("y%d_%d" % (b, h), [HALF], F32, "plane%d" % b if h == 0 else None)
+            nc.scalar.copy(out=y[:], in_=acc[:])
+            nc.vector.tensor_tensor(pages[b][:].indirect(scatter_list[:, list_cols(cols)]), y[:], wgo_sb[:, cols], MULT)
 
-        def quantize_picked(a, h):
-            xg[a, h] = quantize_rows("xg%d_%d" % (a, h), picked[a, h], "xg%d_%d" % (a, h))
+        cq, cr = operand("cq", J), operand("cr", J)
+        wq = [operand("wq%d" % a, N) for a in range(PASSES)]
+        xg = {1: operand("xg1", J)}
+        whole, front, rear = slice(0, J), span(0, HALF), span(1, HALF)
 
         nc.sync.dma_start(gather_list[:], offs)
-        nc.sync.dma_start(out=wgt_sb[0][:], in_=wgt[:, half_cols(0)])
-        for q in range(3):
-            planes[q] = load_plane(q)
-            if q == 0:
-                nc.sync.dma_start(out=wgt_sb[1][:], in_=wgt[:, half_cols(1)])
-            for h in range(HALVES):
-                gather(q, h, planes[q])
-        first_tier(0)
-        planes[3] = load_plane(3)
-        for h in range(HALVES):
-            gather(3, h, planes[3])
-        planes[4] = load_plane(4)
-        gather(4, 0, planes[4])
-        second_tier(0, "cr0")
-        for h in range(HALVES):
-            quantize_picked(0, h)
-        planes[5] = load_plane(5)
-        gather(5, 0, planes[5])
+        plane = load_plane(0)
+        for cols in (front, rear):
+            nc.sync.dma_start(out=wgt_sb[:, cols], in_=wgt[:, cols])
+            gather(0, plane, cols)
+        for q in range(1, PACK):
+            gather(q, load_plane(q), whole)
+
+        c_front = load_rows("c_front", c_rows[:, :, front])
+        xg0_staging = staging("xg0", J)
+        borrowed = xg0_staging[:, QUARTER : QUARTER + HALF, :]
+        weave(borrowed, c_front[:])
+        quantize(cq, front, borrowed)
         nc.sync.dma_start(scatter_list[:], offs2)
-        nc.sync.dma_start(out=wx_sb[:].bitcast(I32), in_=wx_words[0].bitcast(I32))
-        for quad in range(4):
-            nc.sync.dma_start(
-                out=wx_plane[32 * quad : 32 * quad + 4, :].bitcast(I32),
-                in_=wx_scales[0, 4 * quad : 4 * quad + 4, :].bitcast(I32),
-            )
-        weights(0)
-        first_tier(1)
-        for q in range(6, 8):
-            planes[q] = load_plane(q)
-            gather(q, 0, planes[q])
-        quantize_picked(1, 0)
-        weights(1)
-        for q in range(4, 8):
-            gather(q, 1, planes[q])
-        second_tier(1, "wq1")
-        quantize_picked(1, 1)
-        for h in range(HALVES):
-            nc.sync.dma_start(out=wgo_sb[h][:], in_=wgo[:, half_cols(h)])
+        nc.sync.dma_start(out=wx_codes[:].bitcast(I32), in_=wx_words[0].bitcast(I32))
+        for cols in (front, rear):
+            weave(xg0_staging[:, cols, :], picked[0][:, :, cols])
+
+        gather(4, load_plane(4), whole)
+        cr_staging = staging("cr_front", HALF, "plane4")
+        remainder(0, c_front, cr_staging)
+        gather(5, load_plane(5), whole)
+        quantize(cr, front, cr_staging)
+        xg[0] = operand("xg0", J, "plane5")
+        quantize(xg[0], whole, xg0_staging)
+
+        load_wx_scales((0, 1))
+        wt_first = load_rows("wt_first", wt_rows[0])
+        borrowed = as_staging(picked[1][:, 2, :])
+        weave(borrowed, wt_first[:])
+        quantize(wq[0], span(0, N), borrowed)
+        c_rear = load_rows("c_rear", c_rows[:, :, rear])
+        borrowed = as_staging(picked[1][:, 3, :])
+        weave(borrowed, c_rear[:])
+        load_wx_scales((2, 3))
+        gather(6, load_plane(6), whole)
+        quantize(cq, rear, borrowed)
+
+        wt_second = load_rows("wt_second", wt_rows[1])
+        wq1_staging = staging("wq1", N)
+        weave(wq1_staging, wt_second[:])
+        plane = load_plane(7)
+        front_staging = staging("xg1_front", HALF)
+        for s in range(2):
+            cols = span(s, QUARTER)
+            gather(7, plane, cols)
+            weave(front_staging[:, cols, :], picked[1][:, :, cols])
+        gather(7, plane, rear)
+        quantize(wq[1], span(0, N), wq1_staging)
+        quantize(xg[1], front, front_staging)
+
+        cr_staging = staging("cr_rear", HALF, "xg1_front_staging")
+        remainder(1, c_rear, cr_staging)
+        rear_staging = staging("xg1_rear", HALF)
+        weave(rear_staging, picked[1][:, :, rear])
+        quantize(xg[1], rear, rear_staging)
+        quantize(cr, rear, cr_staging)
+
+        nc.sync.dma_start(out=wgo_sb[:], in_=wgo)
         for h in range(HALVES):
             for b in range(BLOCKS):
                 product(b, h)
                 if h == HALVES - 1:
-                    nc.sync.dma_start(out=out[b * P : (b + 1) * P, :], in_=pages[b][:])
+                    nc.sync.dma_start(out=out[span(b, P), :], in_=pages[b][:])

from contextlib import ExitStack

import concourse.mybir as mybir
from concourse.masks import make_identity

K, L, N, T, J = 1024, 512, 512, 2048, 1024
FLOPS = 2 * (K + 2 * L) * N * J

F32 = mybir.dt.float32
BF16 = mybir.dt.bfloat16
I32 = mybir.dt.int32
U32 = mybir.dt.uint32
U16 = mybir.dt.uint16
U8 = mybir.dt.uint8
FP8X4 = mybir.dt.float8_e4m3fn_x4
FP4X4 = mybir.dt.float4_e2m1fn_x4
MULT = mybir.AluOpType.mult
SUBTRACT = mybir.AluOpType.subtract

P = 128
PACK = 4
K_PASS = P * PACK
PASSES = K // K_PASS
HALF = 512
HALVES = J // HALF
QUARTER = HALF // 2
CHUNK = HALF // PACK
CHUNKS = HALF // CHUNK
BLOCKS = N // P
GROUP = 16
QUADRANT = 32
SCALE_ROWS = 4


def span(index, width):
    return slice(index * width, (index + 1) * width)


def tile_list_scat_kernel(
    tc, xT, wgt, wt, c, wx_words, wx_scales, wgo, offs, offs2, out
):
    nc = tc.nc
    with ExitStack() as ctx:
        keep = ctx.enter_context(tc.tile_pool(name="keep", bufs=1))
        psum = ctx.enter_context(tc.psum_pool(name="psum", bufs=1))

        def sbuf(name, shape, dtype, after=None):
            return keep.tile([P] + shape, dtype, name=name, tag=after or name, align_bytes=64)

        def operand(name, width, after=None):
            return sbuf(name + "_codes", [width], U32, after), sbuf(name + "_scales", [width], U8)

        def staging(name, width, after=None):
            return sbuf(name + "_staging", [width, PACK], BF16, after)[:]

        def as_staging(row):
            return row.bitcast(BF16).rearrange("p (w t) -> p w t", t=PACK)

        def walk_rows(rows):
            return rows.rearrange("p t (c i) -> p c t i", i=PACK)

        def walk_staging(staged):
            return staged.rearrange("p (c i) t -> p c t i", i=PACK)

        def weave(staged, rows):
            nc.scalar.copy(out=walk_staging(staged), in_=walk_rows(rows))

        def quantize(dst, cols, staged):
            nc.vector.quantize_mx(
                out=dst[0][:, cols].bitcast(FP8X4), scales=dst[1][:, cols], in_=staged.rearrange("p w t -> p (w t)")
            )

        def list_cols(cols):
            return slice(cols.start // GROUP, cols.stop // GROUP)

        gather_list = sbuf("gather_list", [J // GROUP], U16)
        scatter_list = sbuf("scatter_list", [J // GROUP], U16)
        wgt_sb = sbuf("wgt_sb", [J], F32)
        wgo_sb = sbuf("wgo_sb", [J], F32)
        wx_codes = sbuf("wx_codes", [2 * N], U8)
        wx_plane = sbuf("wx_plane", [N], U8)
        picked = [sbuf("picked%d" % a, [PACK, J], F32) for a in range(PASSES)]
        x_planes = xT.rearrange("(a p t) w -> a t p w", p=P, t=PACK)
        wt_rows = wt.rearrange("(a p t) n -> a p t n", p=P, t=PACK)
        c_rows = c.rearrange("(p t) j -> p t j", t=PACK)

        diagonals = sbuf("diagonals", [2 * PACK - 1, P], BF16)
        nc.vector.memset(diagonals[:], 0.0)
        make_identity(nc, diagonals[:, PACK - 1, :], nomemset=True)
        eye = operand("eye", K_PASS)
        eye_staging = staging("eye", K_PASS)
        for t in range(PACK):
            first = PACK - 1 - t
            nc.scalar.copy(
                out=eye_staging[:, span(t, P), :],
                in_=diagonals[:, first : first + PACK, :].rearrange("p t m -> p m t"),
            )
        quantize(eye, span(0, K_PASS), eye_staging)

        nc.gpsimd.memset(wx_plane[:].bitcast(I32), 0)
        pages = [sbuf("page%d" % b, [T], F32) for b in range(BLOCKS)]
        for page in pages:
            nc.vector.memset(page[:], 0.0)

        def load_plane(q):
            plane = sbuf("plane%d" % q, [T], F32)
            nc.sync.dma_start(out=plane[:], in_=x_planes[q // PACK, q % PACK])
            return plane

        def gather(q, plane, cols):
            nc.vector.tensor_tensor(
                picked[q // PACK][:, q % PACK, cols],
                plane[:].indirect(gather_list[:, list_cols(cols)]),
                wgt_sb[:, cols],
                MULT,
            )

        def load_rows(name, rows):
            tile = sbuf(name, [PACK, HALF], F32)
            nc.sync.dma_start(out=tile[:], in_=rows)
            return tile

        def load_wx_scales(quadrants):
            for quadrant in quadrants:
                start = QUADRANT * quadrant
                nc.sync.dma_start(
                    out=wx_plane[start : start + SCALE_ROWS, :].bitcast(I32),
                    in_=wx_scales[0, span(quadrant, SCALE_ROWS), :].bitcast(I32),
                )

        def remainder(h, c_half, staged):
            for u in range(CHUNKS):
                cols = span(h * CHUNKS + u, CHUNK)
                back = psum.tile([P, PACK, CHUNK], F32, name="back%d_%d" % (h, u), tag="back%d" % u)
                for t in range(PACK):
                    nc.tensor.matmul_mx(
                        out=back[:, t, :],
                        lhsT=eye[0][:, span(t, P)].bitcast(FP8X4),
                        lhsT_scale=eye[1][:, span(t, P)],
                        rhs=cq[0][:, cols].bitcast(FP8X4),
                        rhs_scale=cq[1][:, cols],
                        start=True,
                        stop=True,
                    )
                nc.vector.tensor_tensor(
                    walk_staging(staged[:, span(u, CHUNK), :]),
                    walk_rows(c_half[:, :, span(u, CHUNK)]),
                    walk_rows(back[:]),
                    SUBTRACT,
                )

        def product(b, h):
            rows, cols = span(b, P), span(h, HALF)
            wx_block = (wx_codes[:, span(b, 2 * P)].bitcast(FP4X4), wx_plane[:, rows])
            terms = [(wx_block, cq), (wx_block, cr)]
            for a in range(PASSES):
                terms.append(((wq[a][0][:, rows].bitcast(FP8X4), wq[a][1][:, rows]), xg[a]))
            acc = psum.tile([P, HALF], F32, name="acc%d_%d" % (b, h), tag="acc%d" % b)
            for s, (left, right) in enumerate(terms):
                nc.tensor.matmul_mx(
                    out=acc[:],
                    lhsT=left[0],
                    lhsT_scale=left[1],
                    rhs=right[0][:, cols].bitcast(FP8X4),
                    rhs_scale=right[1][:, cols],
                    start=(s == 0),
                    stop=(s == len(terms) - 1),
                )
            y = sbuf("y%d_%d" % (b, h), [HALF], F32, "plane%d" % b if h == 0 else None)
            nc.scalar.copy(out=y[:], in_=acc[:])
            nc.vector.tensor_tensor(pages[b][:].indirect(scatter_list[:, list_cols(cols)]), y[:], wgo_sb[:, cols], MULT)

        cq, cr = operand("cq", J), operand("cr", J)
        wq = [operand("wq%d" % a, N) for a in range(PASSES)]
        xg = {1: operand("xg1", J)}
        whole, front, rear = slice(0, J), span(0, HALF), span(1, HALF)

        nc.sync.dma_start(gather_list[:], offs)
        plane = load_plane(0)
        for cols in (front, rear):
            nc.sync.dma_start(out=wgt_sb[:, cols], in_=wgt[:, cols])
            gather(0, plane, cols)
        for q in range(1, PACK):
            gather(q, load_plane(q), whole)

        c_front = load_rows("c_front", c_rows[:, :, front])
        xg0_staging = staging("xg0", J)
        borrowed = xg0_staging[:, QUARTER : QUARTER + HALF, :]
        weave(borrowed, c_front[:])
        quantize(cq, front, borrowed)
        nc.sync.dma_start(scatter_list[:], offs2)
        nc.sync.dma_start(out=wx_codes[:].bitcast(I32), in_=wx_words[0].bitcast(I32))
        for cols in (front, rear):
            weave(xg0_staging[:, cols, :], picked[0][:, :, cols])

        gather(4, load_plane(4), whole)
        cr_staging = staging("cr_front", HALF, "plane4")
        remainder(0, c_front, cr_staging)
        gather(5, load_plane(5), whole)
        quantize(cr, front, cr_staging)
        xg[0] = operand("xg0", J, "plane5")
        quantize(xg[0], whole, xg0_staging)

        load_wx_scales((0, 1))
        wt_first = load_rows("wt_first", wt_rows[0])
        borrowed = as_staging(picked[1][:, 2, :])
        weave(borrowed, wt_first[:])
        quantize(wq[0], span(0, N), borrowed)
        c_rear = load_rows("c_rear", c_rows[:, :, rear])
        borrowed = as_staging(picked[1][:, 3, :])
        weave(borrowed, c_rear[:])
        load_wx_scales((2, 3))
        gather(6, load_plane(6), whole)
        quantize(cq, rear, borrowed)

        wt_second = load_rows("wt_second", wt_rows[1])
        wq1_staging = staging("wq1", N)
        weave(wq1_staging, wt_second[:])
        plane = load_plane(7)
        front_staging = staging("xg1_front", HALF)
        for s in range(2):
            cols = span(s, QUARTER)
            gather(7, plane, cols)
            weave(front_staging[:, cols, :], picked[1][:, :, cols])
        gather(7, plane, rear)
        quantize(wq[1], span(0, N), wq1_staging)
        quantize(xg[1], front, front_staging)

        cr_staging = staging("cr_rear", HALF, "xg1_front_staging")
        remainder(1, c_rear, cr_staging)
        rear_staging = staging("xg1_rear", HALF)
        weave(rear_staging, picked[1][:, :, rear])
        quantize(xg[1], rear, rear_staging)
        quantize(cr, rear, cr_staging)

        nc.sync.dma_start(out=wgo_sb[:], in_=wgo)
        for h in range(HALVES):
            for b in range(BLOCKS):
                product(b, h)
                if h == HALVES - 1:
                    nc.sync.dma_start(out=out[span(b, P), :], in_=pages[b][:])
